import numpy as np
import ml_dtypes


def mxq(x, axis, fmt="e4m3"):
    dtype, down = {"e4m3": (ml_dtypes.float8_e4m3fn, 7), "e5m2": (ml_dtypes.float8_e5m2, 14)}[fmt]
    v = np.moveaxis(np.asarray(x, np.float32).astype(ml_dtypes.bfloat16).astype(np.float64), axis, -1)
    blocks = v.reshape(v.shape[:-1] + (-1, 32))
    amax = np.abs(blocks).max(-1, keepdims=True)
    byte = np.maximum(np.where(amax > 0, np.frexp(amax)[1] - 1 + 127, 0) - down, 1)
    scale = np.exp2(byte - 127.0)
    codes = (blocks / scale).astype(np.float32).astype(dtype).astype(np.float64)
    return np.moveaxis((codes * scale).reshape(v.shape), -1, axis)


WIDE = False


def mx_kscale(k):
    if not WIDE:
        return np.ones(k)
    levels = np.array([10, -10, 5, -5, 0])
    if k % 512:
        return np.exp2(np.random.permutation(np.resize(levels, k // 32))).repeat(32)
    a = np.empty((k // 512, 16))
    for p in range(k // 512):
        a[p, :8] = np.random.permutation(np.resize(levels, 8))
        for g in range(8):
            far = levels[np.abs(levels - a[p, g]) >= 10]
            a[p, g + 8] = far[np.random.randint(len(far))]
    return np.exp2(a.ravel()).repeat(32)


def f64(x):
    return np.asarray(x).astype(np.float64)


def striped(idx):
    return np.tile(idx.reshape(-1, 16).T, (8, 1)).astype(np.uint16)


def unstriped(offs):
    return offs[:16].T.reshape(-1).astype(np.int64)


def pack_weight(w):
    k, n = w.shape
    w = f64(np.asarray(w, np.float32).astype(ml_dtypes.bfloat16)).reshape(k // 32, 32, n)
    amax = np.abs(w).max(1)
    byte = np.clip(np.where(amax > 0, np.frexp(amax)[1] - 1 + 127 - 7, 1), 1, 254)
    scaled = (w * np.exp2(127.0 - byte)[:, None, :]).reshape(k, n).astype(np.float32)
    words = np.ascontiguousarray(scaled.reshape(k // 512, 128, 4, n).transpose(0, 1, 3, 2)).astype(ml_dtypes.float8_e4m3fn).view(np.uint8)
    return words, np.ascontiguousarray(byte.astype(np.uint8).reshape(k // 512, 16, n))


def unpack_weight(words, scales):
    g, p, n, _ = words.shape
    vals = np.ascontiguousarray(words).view(ml_dtypes.float8_e4m3fn).astype(np.float64) * np.repeat(np.exp2(scales.astype(np.float64) - 127.0), 8, axis=1)[..., None]
    return vals.transpose(0, 1, 3, 2).reshape(g * 512, n)


def silu(v):
    return v / (1.0 + np.exp(-np.maximum(v, -700.0)))


K, T, S, H, N, U = 512, 2048, 1024, 512, 128, 1024


def setup_inputs():
    n = np.random.standard_normal
    s = mx_kscale(K)[:, None]
    u = mx_kscale(H)
    packed_w3 = pack_weight(n((H, N)) / np.sqrt(H) / u[:, None])
    return {
        "xT": (n((K, T)) * s).astype(np.float32),
        "w1": (n((K, H)) / np.sqrt(2 * K) / s * u).astype(np.float32),
        "w2": (n((K, H)) / np.sqrt(2 * K) / s * u).astype(np.float32),
        "w3_words": packed_w3[0],
        "w3_scales": packed_w3[1],
        "offs": striped(np.random.permutation(T)[:S]),
        "src": striped(np.random.permutation(S)[(S * np.random.uniform(0, 1, U) ** 4).astype(np.int64)]),
        "dst": striped(np.random.permutation(S)),
    }


def reference(xT, w1, w2, w3_words, w3_scales, offs, src, dst):
    xq = mxq(f64(xT)[:, unstriped(offs)], 0, "e4m3")
    y = mxq(f64(w1), 0, "e4m3").T @ xq
    e = mxq(f64(w2), 0, "e4m3").T @ xq
    z = silu(y[:, unstriped(src)] + e[:, unstriped(dst)])
    return unpack_weight(w3_words, w3_scales).T @ mxq(z, 0, "e4m3")

@@ -1,0 +1,179 @@
+from contextlib import ExitStack
+
+import concourse.mybir as mybir
+
+K, T, S, H, N, U = 512, 2048, 1024, 512, 128, 1024
+FLOPS = 2 * K * H * S * 2 + 2 * H * N * U
+
+F32 = mybir.dt.float32
+BF16 = mybir.dt.bfloat16
+I32 = mybir.dt.int32
+U32 = mybir.dt.uint32
+U16 = mybir.dt.uint16
+U8 = mybir.dt.uint8
+FP8X4 = mybir.dt.float8_e4m3fn_x4
+SILU = mybir.ActivationFunctionType.Silu
+ADD = mybir.AluOpType.add
+
+P = 128
+PACK = 4
+LINE = 4
+HALF = 512
+X_CHUNKS = ((0, 1024), (1024, 1536), (1536, 2048))
+EDGE_CHUNKS = ((0, 512), (512, 768), (768, 896), (896, 1024))
+
+
+def tile_picked_hub_silu_e_kernel(tc, xT, w1, w2, w3_words, w3_scales, offs, src, dst, out):
+    nc = tc.nc
+    with ExitStack() as ctx:
+        keep = ctx.enter_context(tc.tile_pool(name="keep", bufs=1))
+        psum = ctx.enter_context(tc.psum_pool(name="psum", bufs=1))
+
+        offs_t = keep.tile([P, S // 16], U16, name="offs_t")
+        src_t = keep.tile([P, U // 16], U16, name="src_t")
+        dst_t = keep.tile([P, U // 16], U16, name="dst_t")
+
+        def entries(tile, lo, hi):
+            return tile[:, lo // 16 : hi // 16]
+
+        warm = keep.tile([P, 2], F32, name="warm")
+        nc.vector.memset(warm[:, 0:1], 0.0)
+        nc.scalar.activation(warm[:, 1:2], warm[:, 0:1], SILU)
+
+        x_rows = xT.rearrange("(p j) t -> p j t", j=PACK)
+        x_raw = {}
+        for u in range(2):
+            for c, (lo, hi) in enumerate(X_CHUNKS):
+                x_raw[u, c] = keep.tile([P, 2, hi - lo], F32, name=f"x_raw{u}{c}")
+                nc.sync.dma_start(out=x_raw[u, c][:], in_=x_rows[:, 2 * u : 2 * u + 2, lo:hi])
+                if (u, c) == (0, 1):
+                    nc.sync.dma_start(offs_t[:], offs)
+        w_raw = {}
+        for a, w in enumerate((w1, w2)):
+            w_rows = w.rearrange("(p j) c -> p j c", j=PACK)
+            for g in range(2):
+                w_raw[a, g] = keep.tile([P, PACK, H // 2], F32, name=f"w_raw{a}{g}")
+                nc.sync.dma_start(out=w_raw[a, g][:], in_=w_rows[:, :, g * (H // 2) : (g + 1) * (H // 2)])
+            nc.sync.dma_start((src_t, dst_t)[a][:], (src, dst)[a])
+        w3_codes = keep.tile([P, N], U32, name="w3_codes", align_bytes=64)
+        w3_bytes = keep.tile([P, N], U8, name="w3_bytes", align_bytes=64)
+        nc.vector.memset(w3_bytes[:].bitcast(I32), 0)
+        nc.sync.dma_start(out=w3_codes[:].bitcast(I32), in_=w3_words[0].rearrange("p n t -> p (n t)").bitcast(I32))
+        for q in range(4):
+            nc.sync.dma_start(out=w3_bytes[32 * q : 32 * q + 4, :].bitcast(I32), in_=w3_scales[0, 4 * q : 4 * q + 4, :].bitcast(I32))
+
+        pairs = [keep.tile([P, T, 2], BF16, name=f"pairs{u}") for u in range(2)]
+        picked = [keep.tile([P, HALF, PACK], BF16, name=f"picked{h}", align_bytes=64) for h in range(2)]
+
+        def cast_x(u, c, copy):
+            lo, hi = X_CHUNKS[c]
+            copy(
+                pairs[u][:, lo:hi, :].rearrange("p (c i) e -> p c e i", i=LINE),
+                x_raw[u, c][:].rearrange("p e (c i) -> p c e i", i=LINE),
+            )
+
+        def gather_x(u, h):
+            window = pairs[u][:].rearrange("p t e -> p (t e)").bitcast(U32)
+            nc.vector.tensor_copy(picked[h][:].bitcast(U32)[:, :, u], window.indirect(entries(offs_t, h * HALF, (h + 1) * HALF)))
+
+        def quantize(values, width, name):
+            codes = keep.tile([P, width], U32, name=f"{name}_codes", align_bytes=64)
+            scales = keep.tile([P, width], U8, name=f"{name}_scales", align_bytes=64)
+            nc.vector.quantize_mx(out=codes[:].bitcast(FP8X4), scales=scales[:], in_=values)
+            return codes, scales
+
+        w_dealt = [keep.tile([P, PACK, P, PACK], BF16, name=f"w_dealt{a}", align_bytes=64) for a in range(2)]
+
+        def cast_w(a):
+            for g in range(2):
+                nc.scalar.copy(
+                    w_dealt[a][:, :, g * (P // 2) : (g + 1) * (P // 2), :].rearrange("p t m j -> p m j t"),
+                    w_raw[a, g][:].rearrange("p j (m t) -> p m j t", t=PACK),
+                )
+
+        def quantize_w(a):
+            return quantize(w_dealt[a][:].rearrange("p t m j -> p (t m j)"), H, f"w{a}")
+
+        def product(bank, lhs, cols, rhs):
+            nc.tensor.matmul_mx(
+                out=bank,
+                lhsT=lhs[0][:, cols].bitcast(FP8X4),
+                lhsT_scale=lhs[1][:, cols],
+                rhs=rhs[0][:].bitcast(FP8X4),
+                rhs_scale=rhs[1][:],
+                start=True,
+                stop=True,
+            )
+
+        for c in range(3):
+            cast_x(0, c, nc.vector.tensor_copy)
+        for h in range(2):
+            gather_x(0, h)
+        cast_x(1, 0, nc.scalar.copy)
+        cast_x(1, 1, nc.scalar.copy)
+        cast_x(1, 2, nc.vector.tensor_copy)
+        cast_w(0)
+
+        rows = [[keep.tile([P, S], F32, name=f"rows{a}{t}") for t in range(PACK)] for a in range(2)]
+        count = [0]
+
+        def first_layer(a, wq, xq, h, t):
+            bank = psum.tile([P, HALF], F32, name="bank", tag=f"bank{count[0] % 6}")
+            count[0] = count[0] + 1
+            product(bank[:], wq, slice(t * P, (t + 1) * P), xq)
+            nc.scalar.copy(rows[a][t][:, h * HALF : (h + 1) * HALF], bank[:])
+
+        gather_x(1, 0)
+        w1q = quantize_w(0)
+        xq = [quantize(picked[0][:].rearrange("p n j -> p (n j)"), HALF, "x0")]
+        gather_x(1, 1)
+        for t in range(PACK):
+            first_layer(0, w1q, xq[0], 0, t)
+        xq.append(quantize(picked[1][:].rearrange("p n j -> p (n j)"), HALF, "x1"))
+        for t in range(PACK):
+            first_layer(0, w1q, xq[1], 1, t)
+        cast_w(1)
+
+        fetched = [keep.tile([P, U], F32, name=f"fetched{t}") for t in range(PACK)]
+
+        def fetch_sources(t):
+            for h in range(2):
+                nc.vector.tensor_copy(fetched[t][:, h * HALF : (h + 1) * HALF], rows[0][t][:].indirect(entries(src_t, h * HALF, (h + 1) * HALF)))
+
+        fetch_sources(0)
+        fetch_sources(1)
+        w2q = quantize_w(1)
+        for t in range(PACK):
+            for h in range(2):
+                first_layer(1, w2q, xq[h], h, t)
+        fetch_sources(2)
+        fetch_sources(3)
+
+        def join(c):
+            lo, hi = EDGE_CHUNKS[c]
+            sums = keep.tile([P, PACK, hi - lo], F32, name=f"sums{c}")
+            for t in range(PACK):
+                nc.vector.tensor_tensor(sums[:, t, :], rows[1][t][:].indirect(entries(dst_t, lo, hi)), fetched[t][:, lo:hi], ADD)
+            z = keep.tile([P, hi - lo, PACK], BF16, name=f"z{c}", align_bytes=64)
+            nc.scalar.activation(
+                z[:].rearrange("p (c i) t -> p c t i", i=LINE),
+                sums[:].rearrange("p t (c i) -> p c t i", i=LINE),
+                SILU,
+            )
+            return z
+
+        def second_layer(c, z):
+            lo, hi = EDGE_CHUNKS[c]
+            zq = quantize(z[:].rearrange("p n j -> p (n j)"), hi - lo, f"z{c}")
+            bank = psum.tile([P, hi - lo], F32, name="out_bank", tag=f"out_bank{c % 2}")
+            product(bank[:], (w3_codes, w3_bytes), slice(0, N), zq)
+            result = keep.tile([P, hi - lo], F32, name=f"result{c}")
+            nc.scalar.copy(result[:], bank[:])
+            nc.sync.dma_start(out=out[:, lo:hi], in_=result[:])
+
+        z_prev = join(0)
+        for c in range(1, len(EDGE_CHUNKS)):
+            z_now = join(c)
+            second_layer(c - 1, z_prev)
+            z_prev = z_now
+        second_layer(len(EDGE_CHUNKS) - 1, z_prev)

@@ -19,7 +19,10 @@ P = 128
 PACK = 4
 LINE = 4
 HALF = 512
-X_CHUNKS = ((0, 1024), (1024, 1536), (1536, 2048))
+X_CHUNKS = (
+    ((0, 1024), (1024, 2048)),
+    ((0, 1024), (1024, 1536), (1536, 2048)),
+)
 EDGE_CHUNKS = ((0, 512), (512, 768), (768, 896), (896, 1024))
 
 
@@ -43,7 +46,7 @@ def tile_picked_hub_silu_e_kernel(tc, xT, w1, w2, w3_words, w3_scales, offs, src
         x_rows = xT.rearrange("(p j) t -> p j t", j=PACK)
         x_raw = {}
         for u in range(2):
-            for c, (lo, hi) in enumerate(X_CHUNKS):
+            for c, (lo, hi) in enumerate(X_CHUNKS[u]):
                 x_raw[u, c] = keep.tile([P, 2, hi - lo], F32, name=f"x_raw{u}{c}")
                 nc.sync.dma_start(out=x_raw[u, c][:], in_=x_rows[:, 2 * u : 2 * u + 2, lo:hi])
                 if (u, c) == (0, 1):
@@ -51,10 +54,10 @@ def tile_picked_hub_silu_e_kernel(tc, xT, w1, w2, w3_words, w3_scales, offs, src
         w_raw = {}
         for a, w in enumerate((w1, w2)):
             w_rows = w.rearrange("(p j) c -> p j c", j=PACK)
-            for g in range(2):
-                w_raw[a, g] = keep.tile([P, PACK, H // 2], F32, name=f"w_raw{a}{g}")
-                nc.sync.dma_start(out=w_raw[a, g][:], in_=w_rows[:, :, g * (H // 2) : (g + 1) * (H // 2)])
-            nc.sync.dma_start((src_t, dst_t)[a][:], (src, dst)[a])
+            w_raw[a] = keep.tile([P, PACK, H], F32, name=f"w_raw{a}")
+            nc.sync.dma_start(out=w_raw[a][:], in_=w_rows)
+        nc.sync.dma_start(src_t[:], src)
+        nc.sync.dma_start(dst_t[:], dst)
         w3_codes = keep.tile([P, N], U32, name="w3_codes", align_bytes=64)
         w3_bytes = keep.tile([P, N], U8, name="w3_bytes", align_bytes=64)
         nc.vector.memset(w3_bytes[:].bitcast(I32), 0)
@@ -63,36 +66,35 @@ def tile_picked_hub_silu_e_kernel(tc, xT, w1, w2, w3_words, w3_scales, offs, src
             nc.sync.dma_start(out=w3_bytes[32 * q : 32 * q + 4, :].bitcast(I32), in_=w3_scales[0, 4 * q : 4 * q + 4, :].bitcast(I32))
 
         pairs = [keep.tile([P, T, 2], BF16, name=f"pairs{u}") for u in range(2)]
-        picked = [keep.tile([P, HALF, PACK], BF16, name=f"picked{h}", align_bytes=64) for h in range(2)]
+        picked = [keep.tile([P, HALF, PACK], BF16, name=f"picked{h}", tag=f"picked{h}", align_bytes=64) for h in range(2)]
 
-        def cast_x(u, c, copy):
-            lo, hi = X_CHUNKS[c]
+        def cast_x(u, c, copy, first, last):
+            lo = X_CHUNKS[u][c][0]
             copy(
-                pairs[u][:, lo:hi, :].rearrange("p (c i) e -> p c e i", i=LINE),
-                x_raw[u, c][:].rearrange("p e (c i) -> p c e i", i=LINE),
+                pairs[u][:, lo + first : lo + last, :].rearrange("p (c i) e -> p c e i", i=LINE),
+                x_raw[u, c][:, :, first:last].rearrange("p e (c i) -> p c e i", i=LINE),
             )
 
         def gather_x(u, h):
             window = pairs[u][:].rearrange("p t e -> p (t e)").bitcast(U32)
             nc.vector.tensor_copy(picked[h][:].bitcast(U32)[:, :, u], window.indirect(entries(offs_t, h * HALF, (h + 1) * HALF)))
 
-        def quantize(values, width, name):
-            codes = keep.tile([P, width], U32, name=f"{name}_codes", align_bytes=64)
+        def quantize(values, width, name, slot=None):
+            codes = keep.tile([P, width], U32, name=f"{name}_codes", tag=slot or f"{name}_codes", align_bytes=64)
             scales = keep.tile([P, width], U8, name=f"{name}_scales", align_bytes=64)
             nc.vector.quantize_mx(out=codes[:].bitcast(FP8X4), scales=scales[:], in_=values)
             return codes, scales
 
-        w_dealt = [keep.tile([P, PACK, P, PACK], BF16, name=f"w_dealt{a}", align_bytes=64) for a in range(2)]
+        def cast_w(a, lo, hi, slot, copy):
+            dealt = keep.tile([P, hi - lo, P, PACK], BF16, name=f"w_dealt{a}{lo}", tag=slot, align_bytes=64)
+            copy(
+                dealt[:].rearrange("p t m j -> p m j t"),
+                w_raw[a][:].rearrange("p j (m t) -> p m j t", t=PACK)[:, :, :, lo:hi],
+            )
+            return dealt
 
-        def cast_w(a):
-            for g in range(2):
-                nc.scalar.copy(
-                    w_dealt[a][:, :, g * (P // 2) : (g + 1) * (P // 2), :].rearrange("p t m j -> p m j t"),
-                    w_raw[a, g][:].rearrange("p j (m t) -> p m j t", t=PACK),
-                )
-
-        def quantize_w(a):
-            return quantize(w_dealt[a][:].rearrange("p t m j -> p (t m j)"), H, f"w{a}")
+        def quantize_w(dealt, lo, hi, name, slot=None):
+            return quantize(dealt[:, lo:hi].rearrange("p t m j -> p (t m j)"), (hi - lo) * P, name, slot)
 
         def product(bank, lhs, cols, rhs):
             nc.tensor.matmul_mx(
@@ -105,59 +107,63 @@ def tile_picked_hub_silu_e_kernel(tc, xT, w1, w2, w3_words, w3_scales, offs, src
                 stop=True,
             )
 
-        for c in range(3):
-            cast_x(0, c, nc.vector.tensor_copy)
+        cast_x(0, 0, nc.vector.tensor_copy, 0, 1024)
+        cast_x(0, 1, nc.vector.tensor_copy, 0, 640)
+        cast_x(0, 1, nc.scalar.copy, 640, 1024)
         for h in range(2):
             gather_x(0, h)
-        cast_x(1, 0, nc.scalar.copy)
-        cast_x(1, 1, nc.scalar.copy)
-        cast_x(1, 2, nc.vector.tensor_copy)
-        cast_w(0)
+        cast_x(1, 0, nc.scalar.copy, 0, 1024)
+        cast_x(1, 1, nc.vector.tensor_copy, 0, 512)
+        cast_x(1, 2, nc.vector.tensor_copy, 0, 320)
+        cast_x(1, 2, nc.scalar.copy, 320, 512)
+        w1_first = cast_w(0, 0, 1, "slot_a", nc.scalar.copy)
+        w1_second = cast_w(0, 1, 2, "w1_second", nc.scalar.copy)
 
         rows = [[keep.tile([P, S], F32, name=f"rows{a}{t}") for t in range(PACK)] for a in range(2)]
         count = [0]
 
-        def first_layer(a, wq, xq, h, t):
-            bank = psum.tile([P, HALF], F32, name="bank", tag=f"bank{count[0] % 6}")
-            count[0] = count[0] + 1
-            product(bank[:], wq, slice(t * P, (t + 1) * P), xq)
-            nc.scalar.copy(rows[a][t][:, h * HALF : (h + 1) * HALF], bank[:])
+        def first_layer(a, wq, first, t):
+            for h in range(2):
+                bank = psum.tile([P, HALF], F32, name="bank", tag=f"bank{count[0] % 8}")
+                count[0] = count[0] + 1
+                product(bank[:], wq, slice((t - first) * P, (t - first + 1) * P), xq[h])
+                nc.scalar.copy(rows[a][t][:, h * HALF : (h + 1) * HALF], bank[:])
 
         gather_x(1, 0)
-        w1q = quantize_w(0)
-        xq = [quantize(picked[0][:].rearrange("p n j -> p (n j)"), HALF, "x0")]
         gather_x(1, 1)
-        for t in range(PACK):
-            first_layer(0, w1q, xq[0], 0, t)
-        xq.append(quantize(picked[1][:].rearrange("p n j -> p (n j)"), HALF, "x1"))
-        for t in range(PACK):
-            first_layer(0, w1q, xq[1], 1, t)
-        cast_w(1)
+        xq = [quantize(picked[0][:].rearrange("p n j -> p (n j)"), HALF, "x0")]
+        w1q = [quantize_w(w1_first, 0, 1, "w10")]
+        xq.append(quantize(picked[1][:].rearrange("p n j -> p (n j)"), HALF, "x1", "slot_a"))
+        w1q.append(quantize_w(w1_second, 0, 1, "w11", "slot_b"))
+        w1_rest = cast_w(0, 2, PACK, "picked1", nc.vector.tensor_copy)
+        w1q.append(quantize_w(w1_rest, 0, 2, "w12"))
+        first_layer(0, w1q[0], 0, 0)
+        first_layer(0, w1q[1], 1, 1)
+        w2_dealt = cast_w(1, 0, PACK, "slot_b", nc.scalar.copy)
+        first_layer(0, w1q[2], 2, 2)
+        first_layer(0, w1q[2], 2, 3)
 
-        fetched = [keep.tile([P, U], F32, name=f"fetched{t}") for t in range(PACK)]
+        fetched = [[keep.tile([P, HALF], F32, name=f"fetched{t}{h}", tag=f"fetched{t}{h}") for h in range(2)] for t in range(PACK)]
 
         def fetch_sources(t):
             for h in range(2):
-                nc.vector.tensor_copy(fetched[t][:, h * HALF : (h + 1) * HALF], rows[0][t][:].indirect(entries(src_t, h * HALF, (h + 1) * HALF)))
+                nc.vector.tensor_copy(fetched[t][h][:], rows[0][t][:].indirect(entries(src_t, h * HALF, (h + 1) * HALF)))
 
         fetch_sources(0)
         fetch_sources(1)
-        w2q = quantize_w(1)
+        w2q = quantize_w(w2_dealt, 0, PACK, "w2")
         for t in range(PACK):
-            for h in range(2):
-                first_layer(1, w2q, xq[h], h, t)
+            first_layer(1, w2q, 0, t)
         fetch_sources(2)
         fetch_sources(3)
-
-        def join(c):
+        def join(c, sums):
             lo, hi = EDGE_CHUNKS[c]
-            sums = keep.tile([P, PACK, hi - lo], F32, name=f"sums{c}")
             for t in range(PACK):
-                nc.vector.tensor_tensor(sums[:, t, :], rows[1][t][:].indirect(entries(dst_t, lo, hi)), fetched[t][:, lo:hi], ADD)
-            z = keep.tile([P, hi - lo, PACK], BF16, name=f"z{c}", align_bytes=64)
+                nc.vector.tensor_tensor(sums[:, t, :], rows[1][t][:].indirect(entries(dst_t, lo, hi)), fetched[t][lo // HALF][:, lo % HALF : lo % HALF + hi - lo], ADD)
+            z = keep.tile([P, hi - lo, PACK], BF16, name=f"z{c}", tag="z0_codes" if c == 3 else f"z{c}", align_bytes=64)
             nc.scalar.activation(
                 z[:].rearrange("p (c i) t -> p c t i", i=LINE),
-                sums[:].rearrange("p t (c i) -> p c t i", i=LINE),
+                sums.rearrange("p t (c i) -> p c t i", i=LINE),
                 SILU,
             )
             return z
@@ -165,15 +171,20 @@ def tile_picked_hub_silu_e_kernel(tc, xT, w1, w2, w3_words, w3_scales, offs, src
         def second_layer(c, z):
             lo, hi = EDGE_CHUNKS[c]
             zq = quantize(z[:].rearrange("p n j -> p (n j)"), hi - lo, f"z{c}")
-            bank = psum.tile([P, hi - lo], F32, name="out_bank", tag=f"out_bank{c % 2}")
+            bank = psum.tile([P, hi - lo], F32, name="out_bank", tag=f"bank{c}")
             product(bank[:], (w3_codes, w3_bytes), slice(0, N), zq)
             result = keep.tile([P, hi - lo], F32, name=f"result{c}")
             nc.scalar.copy(result[:], bank[:])
             nc.sync.dma_start(out=out[:, lo:hi], in_=result[:])
 
-        z_prev = join(0)
-        for c in range(1, len(EDGE_CHUNKS)):
-            z_now = join(c)
-            second_layer(c - 1, z_prev)
-            z_prev = z_now
-        second_layer(len(EDGE_CHUNKS) - 1, z_prev)
+        sums0 = keep.tile([P, PACK, 512], F32, name="sums0")
+        z0 = join(0, sums0[:])
+        sums12 = keep.tile([P, PACK * 384], F32, name="sums12", tag="fetched30")
+        z1 = join(1, sums12[:, 0 : PACK * 256].rearrange("p (t n) -> p t n", t=PACK))
+        z2 = join(2, sums12[:, PACK * 256 :].rearrange("p (t n) -> p t n", t=PACK))
+        second_layer(0, z0)
+        sums3 = keep.tile([P, PACK, 128], F32, name="sums3", tag="z0", align_bytes=64)
+        z3 = join(3, sums3[:])
+        second_layer(1, z1)
+        second_layer(2, z2)
+        second_layer(3, z3)

@@ -24,6 +24,7 @@ X_CHUNKS = (
     ((0, 1024), (1024, 1536), (1536, 2048)),
 )
 EDGE_CHUNKS = ((0, 512), (512, 768), (768, 896), (896, 1024))
+JOIN_CHUNKS = ((0, 512), (512, 800), (800, 960), (960, 1024))
 
 
 def tile_picked_hub_silu_e_kernel(tc, xT, w1, w2, w3_words, w3_scales, offs, src, dst, out):
@@ -66,6 +67,7 @@ def tile_picked_hub_silu_e_kernel(tc, xT, w1, w2, w3_words, w3_scales, offs, src
             nc.sync.dma_start(out=w3_bytes[32 * q : 32 * q + 4, :].bitcast(I32), in_=w3_scales[0, 4 * q : 4 * q + 4, :].bitcast(I32))
 
         pairs = [keep.tile([P, T, 2], BF16, name=f"pairs{u}") for u in range(2)]
+        loose = keep.tile([P, 2, HALF], U32, name="loose")
         picked = [keep.tile([P, HALF, PACK], BF16, name=f"picked{h}", tag=f"picked{h}", align_bytes=64) for h in range(2)]
 
         def cast_x(u, c, copy, first, last):
@@ -75,14 +77,16 @@ def tile_picked_hub_silu_e_kernel(tc, xT, w1, w2, w3_words, w3_scales, offs, src
                 x_raw[u, c][:, :, first:last].rearrange("p e (c i) -> p c e i", i=LINE),
             )
 
-        def gather_x(u, h):
+        def gather_x(u, h, lo=0, hi=HALF):
             window = pairs[u][:].rearrange("p t e -> p (t e)").bitcast(U32)
-            nc.vector.tensor_copy(picked[h][:].bitcast(U32)[:, :, u], window.indirect(entries(offs_t, h * HALF, (h + 1) * HALF)))
+            nc.vector.tensor_copy(picked[h][:].bitcast(U32)[:, lo:hi, u] if h else loose[:, u, lo:hi], window.indirect(entries(offs_t, h * HALF + lo, h * HALF + hi)))
 
-        def quantize(values, width, name, slot=None):
+        def quantize(values, width, name, slot=None, parts=1):
             codes = keep.tile([P, width], U32, name=f"{name}_codes", tag=slot or f"{name}_codes", align_bytes=64)
             scales = keep.tile([P, width], U8, name=f"{name}_scales", align_bytes=64)
-            nc.vector.quantize_mx(out=codes[:].bitcast(FP8X4), scales=scales[:], in_=values)
+            step = width // parts
+            for lo in range(0, width, step):
+                nc.vector.quantize_mx(out=codes[:, lo : lo + step].bitcast(FP8X4), scales=scales[:, lo : lo + step], in_=values[:, PACK * lo : PACK * (lo + step)])
             return codes, scales
 
         def cast_w(a, lo, hi, slot, copy):
@@ -96,13 +100,13 @@ def tile_picked_hub_silu_e_kernel(tc, xT, w1, w2, w3_words, w3_scales, offs, src
         def quantize_w(dealt, lo, hi, name, slot=None):
             return quantize(dealt[:, lo:hi].rearrange("p t m j -> p (t m j)"), (hi - lo) * P, name, slot)
 
-        def product(bank, lhs, cols, rhs):
+        def product(bank, lhs, cols, rhs, lo, hi):
             nc.tensor.matmul_mx(
                 out=bank,
                 lhsT=lhs[0][:, cols].bitcast(FP8X4),
                 lhsT_scale=lhs[1][:, cols],
-                rhs=rhs[0][:].bitcast(FP8X4),
-                rhs_scale=rhs[1][:],
+                rhs=rhs[0][:, lo:hi].bitcast(FP8X4),
+                rhs_scale=rhs[1][:, lo:hi],
                 start=True,
                 stop=True,
             )
@@ -116,20 +120,25 @@ def tile_picked_hub_silu_e_kernel(tc, xT, w1, w2, w3_words, w3_scales, offs, src
         cast_x(1, 1, nc.vector.tensor_copy, 0, 512)
         cast_x(1, 2, nc.vector.tensor_copy, 0, 320)
         cast_x(1, 2, nc.scalar.copy, 320, 512)
+        for lo in (0, 256):
+            gather_x(1, 0, lo, lo + 256)
+            nc.scalar.copy(
+                picked[0][:].bitcast(U32)[:, lo : lo + 256].rearrange("p (c i) u -> p c u i", i=LINE),
+                loose[:, :, lo : lo + 256].rearrange("p u (c i) -> p c u i", i=LINE),
+            )
         w1_first = cast_w(0, 0, 1, "slot_a", nc.scalar.copy)
         w1_second = cast_w(0, 1, 2, "w1_second", nc.scalar.copy)
 
         rows = [[keep.tile([P, S], F32, name=f"rows{a}{t}") for t in range(PACK)] for a in range(2)]
         count = [0]
 
-        def first_layer(a, wq, first, t):
-            for h in range(2):
-                bank = psum.tile([P, HALF], F32, name="bank", tag=f"bank{count[0] % 8}")
+        def first_layer(a, wq, first, t, pieces=((0, 0, HALF, nc.scalar.copy), (1, 0, HALF, nc.scalar.copy))):
+            for h, lo, hi, copy in pieces:
+                bank = psum.tile([P, hi - lo], F32, name="bank", tag=f"bank{count[0] % 8}")
                 count[0] = count[0] + 1
-                product(bank[:], wq, slice((t - first) * P, (t - first + 1) * P), xq[h])
-                nc.scalar.copy(rows[a][t][:, h * HALF : (h + 1) * HALF], bank[:])
+                product(bank[:], wq, slice((t - first) * P, (t - first + 1) * P), xq[h], lo, hi)
+                copy(rows[a][t][:, h * HALF + lo : h * HALF + hi], bank[:])
 
-        gather_x(1, 0)
         gather_x(1, 1)
         xq = [quantize(picked[0][:].rearrange("p n j -> p (n j)"), HALF, "x0")]
         w1q = [quantize_w(w1_first, 0, 1, "w10")]
@@ -157,34 +166,42 @@ def tile_picked_hub_silu_e_kernel(tc, xT, w1, w2, w3_words, w3_scales, offs, src
         fetch_sources(2)
         fetch_sources(3)
         def join(c, sums):
-            lo, hi = EDGE_CHUNKS[c]
+            lo, hi = JOIN_CHUNKS[c]
             for t in range(PACK):
                 nc.vector.tensor_tensor(sums[:, t, :], rows[1][t][:].indirect(entries(dst_t, lo, hi)), fetched[t][lo // HALF][:, lo % HALF : lo % HALF + hi - lo], ADD)
-            z = keep.tile([P, hi - lo, PACK], BF16, name=f"z{c}", tag="z0_codes" if c == 3 else f"z{c}", align_bytes=64)
+
+        def activate(z, sums):
             nc.scalar.activation(
-                z[:].rearrange("p (c i) t -> p c t i", i=LINE),
+                z.rearrange("p (c i) t -> p c t i", i=LINE),
                 sums.rearrange("p t (c i) -> p c t i", i=LINE),
                 SILU,
             )
-            return z
 
         def second_layer(c, z):
             lo, hi = EDGE_CHUNKS[c]
-            zq = quantize(z[:].rearrange("p n j -> p (n j)"), hi - lo, f"z{c}")
+            zq = quantize(z.rearrange("p n j -> p (n j)"), hi - lo, f"z{c}")
             bank = psum.tile([P, hi - lo], F32, name="out_bank", tag=f"bank{c}")
-            product(bank[:], (w3_codes, w3_bytes), slice(0, N), zq)
+            product(bank[:], (w3_codes, w3_bytes), slice(0, N), zq, 0, hi - lo)
             result = keep.tile([P, hi - lo], F32, name=f"result{c}")
             nc.scalar.copy(result[:], bank[:])
             nc.sync.dma_start(out=out[:, lo:hi], in_=result[:])
 
         sums0 = keep.tile([P, PACK, 512], F32, name="sums0")
-        z0 = join(0, sums0[:])
-        sums12 = keep.tile([P, PACK * 384], F32, name="sums12", tag="fetched30")
-        z1 = join(1, sums12[:, 0 : PACK * 256].rearrange("p (t n) -> p t n", t=PACK))
-        z2 = join(2, sums12[:, PACK * 256 :].rearrange("p (t n) -> p t n", t=PACK))
-        second_layer(0, z0)
-        sums3 = keep.tile([P, PACK, 128], F32, name="sums3", tag="z0", align_bytes=64)
-        z3 = join(3, sums3[:])
-        second_layer(1, z1)
-        second_layer(2, z2)
-        second_layer(3, z3)
+        z0 = keep.tile([P, 512, PACK], BF16, name="z0", tag="z0", align_bytes=64)
+        join(0, sums0[:])
+        activate(z0[:], sums0[:])
+        sums1 = keep.tile([P, PACK, 288], F32, name="sums1", tag="fetched30")
+        z_rest = keep.tile([P, 512, PACK], BF16, name="z_rest", align_bytes=64)
+        join(1, sums1[:])
+        activate(z_rest[:, 0:288], sums1[:])
+        second_layer(0, z0[:])
+        sums23 = keep.tile([P, PACK * 224], F32, name="sums23", tag="z0", align_bytes=64)
+        sums2 = sums23[:, 0 : PACK * 160].rearrange("p (t n) -> p t n", t=PACK)
+        sums3 = sums23[:, PACK * 160 :].rearrange("p (t n) -> p t n", t=PACK)
+        join(2, sums2)
+        activate(z_rest[:, 288:448], sums2)
+        join(3, sums3)
+        activate(z_rest[:, 448:512], sums3)
+        second_layer(1, z_rest[:, 0:256])
+        second_layer(2, z_rest[:, 256:384])
+        second_layer(3, z_rest[:, 384:512])

from contextlib import ExitStack

import concourse.mybir as mybir

K, T, S, H, N, U = 512, 2048, 1024, 512, 128, 1024
FLOPS = 2 * K * H * S * 2 + 2 * H * N * U

F32 = mybir.dt.float32
BF16 = mybir.dt.bfloat16
I32 = mybir.dt.int32
U32 = mybir.dt.uint32
U16 = mybir.dt.uint16
U8 = mybir.dt.uint8
FP8X4 = mybir.dt.float8_e4m3fn_x4
SILU = mybir.ActivationFunctionType.Silu
ADD = mybir.AluOpType.add

P = 128
PACK = 4
LINE = 4
HALF = 512
X_CHUNKS = (
    ((0, 1024), (1024, 2048)),
    ((0, 1024), (1024, 1536), (1536, 2048)),
)
EDGE_CHUNKS = ((0, 512), (512, 768), (768, 896), (896, 1024))
JOIN_CHUNKS = ((0, 512), (512, 800), (800, 960), (960, 1024))


def tile_picked_hub_silu_e_kernel(tc, xT, w1, w2, w3_words, w3_scales, offs, src, dst, out):
    nc = tc.nc
    with ExitStack() as ctx:
        keep = ctx.enter_context(tc.tile_pool(name="keep", bufs=1))
        psum = ctx.enter_context(tc.psum_pool(name="psum", bufs=1))

        offs_t = keep.tile([P, S // 16], U16, name="offs_t")
        src_t = keep.tile([P, U // 16], U16, name="src_t")
        dst_t = keep.tile([P, U // 16], U16, name="dst_t")

        def entries(tile, lo, hi):
            return tile[:, lo // 16 : hi // 16]

        warm = keep.tile([P, 2], F32, name="warm")
        nc.vector.memset(warm[:, 0:1], 0.0)
        nc.scalar.activation(warm[:, 1:2], warm[:, 0:1], SILU)

        x_rows = xT.rearrange("(p j) t -> p j t", j=PACK)
        x_raw = {}
        for u in range(2):
            for c, (lo, hi) in enumerate(X_CHUNKS[u]):
                x_raw[u, c] = keep.tile([P, 2, hi - lo], F32, name=f"x_raw{u}{c}")
                nc.sync.dma_start(out=x_raw[u, c][:], in_=x_rows[:, 2 * u : 2 * u + 2, lo:hi])
                if (u, c) == (0, 1):
                    nc.sync.dma_start(offs_t[:], offs)
        w_raw = {}
        for a, w in enumerate((w1, w2)):
            w_rows = w.rearrange("(p j) c -> p j c", j=PACK)
            w_raw[a] = keep.tile([P, PACK, H], F32, name=f"w_raw{a}")
            nc.sync.dma_start(out=w_raw[a][:], in_=w_rows)
        nc.sync.dma_start(src_t[:], src)
        nc.sync.dma_start(dst_t[:], dst)
        w3_codes = keep.tile([P, N], U32, name="w3_codes", align_bytes=64)
        w3_bytes = keep.tile([P, N], U8, name="w3_bytes", align_bytes=64)
        nc.vector.memset(w3_bytes[:].bitcast(I32), 0)
        nc.sync.dma_start(out=w3_codes[:].bitcast(I32), in_=w3_words[0].rearrange("p n t -> p (n t)").bitcast(I32))
        for q in range(4):
            nc.sync.dma_start(out=w3_bytes[32 * q : 32 * q + 4, :].bitcast(I32), in_=w3_scales[0, 4 * q : 4 * q + 4, :].bitcast(I32))

        pairs = [keep.tile([P, T, 2], BF16, name=f"pairs{u}") for u in range(2)]
        loose = keep.tile([P, 2, HALF], U32, name="loose")
        picked = [keep.tile([P, HALF, PACK], BF16, name=f"picked{h}", tag=f"picked{h}", align_bytes=64) for h in range(2)]

        def cast_x(u, c, copy, first, last):
            lo = X_CHUNKS[u][c][0]
            copy(
                pairs[u][:, lo + first : lo + last, :].rearrange("p (c i) e -> p c e i", i=LINE),
                x_raw[u, c][:, :, first:last].rearrange("p e (c i) -> p c e i", i=LINE),
            )

        def gather_x(u, h, lo=0, hi=HALF):
            window = pairs[u][:].rearrange("p t e -> p (t e)").bitcast(U32)
            nc.vector.tensor_copy(picked[h][:].bitcast(U32)[:, lo:hi, u] if h else loose[:, u, lo:hi], window.indirect(entries(offs_t, h * HALF + lo, h * HALF + hi)))

        def quantize(values, width, name, slot=None, parts=1):
            codes = keep.tile([P, width], U32, name=f"{name}_codes", tag=slot or f"{name}_codes", align_bytes=64)
            scales = keep.tile([P, width], U8, name=f"{name}_scales", align_bytes=64)
            step = width // parts
            for lo in range(0, width, step):
                nc.vector.quantize_mx(out=codes[:, lo : lo + step].bitcast(FP8X4), scales=scales[:, lo : lo + step], in_=values[:, PACK * lo : PACK * (lo + step)])
            return codes, scales

        def cast_w(a, lo, hi, slot, copy):
            dealt = keep.tile([P, hi - lo, P, PACK], BF16, name=f"w_dealt{a}{lo}", tag=slot, align_bytes=64)
            copy(
                dealt[:].rearrange("p t m j -> p m j t"),
                w_raw[a][:].rearrange("p j (m t) -> p m j t", t=PACK)[:, :, :, lo:hi],
            )
            return dealt

        def quantize_w(dealt, lo, hi, name, slot=None):
            return quantize(dealt[:, lo:hi].rearrange("p t m j -> p (t m j)"), (hi - lo) * P, name, slot)

        def product(bank, lhs, cols, rhs, lo, hi):
            nc.tensor.matmul_mx(
                out=bank,
                lhsT=lhs[0][:, cols].bitcast(FP8X4),
                lhsT_scale=lhs[1][:, cols],
                rhs=rhs[0][:, lo:hi].bitcast(FP8X4),
                rhs_scale=rhs[1][:, lo:hi],
                start=True,
                stop=True,
            )

        cast_x(0, 0, nc.vector.tensor_copy, 0, 1024)
        cast_x(0, 1, nc.vector.tensor_copy, 0, 640)
        cast_x(0, 1, nc.scalar.copy, 640, 1024)
        for h in range(2):
            gather_x(0, h)
        cast_x(1, 0, nc.scalar.copy, 0, 1024)
        cast_x(1, 1, nc.vector.tensor_copy, 0, 512)
        cast_x(1, 2, nc.vector.tensor_copy, 0, 320)
        cast_x(1, 2, nc.scalar.copy, 320, 512)
        for lo in (0, 256):
            gather_x(1, 0, lo, lo + 256)
            nc.scalar.copy(
                picked[0][:].bitcast(U32)[:, lo : lo + 256].rearrange("p (c i) u -> p c u i", i=LINE),
                loose[:, :, lo : lo + 256].rearrange("p u (c i) -> p c u i", i=LINE),
            )
        w1_first = cast_w(0, 0, 1, "slot_a", nc.scalar.copy)
        w1_second = cast_w(0, 1, 2, "w1_second", nc.scalar.copy)

        rows = [[keep.tile([P, S], F32, name=f"rows{a}{t}") for t in range(PACK)] for a in range(2)]
        count = [0]

        def first_layer(a, wq, first, t, pieces=((0, 0, HALF, nc.scalar.copy), (1, 0, HALF, nc.scalar.copy))):
            for h, lo, hi, copy in pieces:
                bank = psum.tile([P, hi - lo], F32, name="bank", tag=f"bank{count[0] % 8}")
                count[0] = count[0] + 1
                product(bank[:], wq, slice((t - first) * P, (t - first + 1) * P), xq[h], lo, hi)
                copy(rows[a][t][:, h * HALF + lo : h * HALF + hi], bank[:])

        gather_x(1, 1)
        xq = [quantize(picked[0][:].rearrange("p n j -> p (n j)"), HALF, "x0")]
        w1q = [quantize_w(w1_first, 0, 1, "w10")]
        xq.append(quantize(picked[1][:].rearrange("p n j -> p (n j)"), HALF, "x1", "slot_a"))
        w1q.append(quantize_w(w1_second, 0, 1, "w11", "slot_b"))
        w1_rest = cast_w(0, 2, PACK, "picked1", nc.vector.tensor_copy)
        w1q.append(quantize_w(w1_rest, 0, 2, "w12"))
        first_layer(0, w1q[0], 0, 0)
        first_layer(0, w1q[1], 1, 1)
        w2_dealt = cast_w(1, 0, PACK, "slot_b", nc.scalar.copy)
        first_layer(0, w1q[2], 2, 2)
        first_layer(0, w1q[2], 2, 3)

        fetched = [[keep.tile([P, HALF], F32, name=f"fetched{t}{h}", tag=f"fetched{t}{h}") for h in range(2)] for t in range(PACK)]

        def fetch_sources(t):
            for h in range(2):
                nc.vector.tensor_copy(fetched[t][h][:], rows[0][t][:].indirect(entries(src_t, h * HALF, (h + 1) * HALF)))

        fetch_sources(0)
        fetch_sources(1)
        w2q = quantize_w(w2_dealt, 0, PACK, "w2")
        for t in range(PACK):
            first_layer(1, w2q, 0, t)
        fetch_sources(2)
        fetch_sources(3)
        def join(c, sums):
            lo, hi = JOIN_CHUNKS[c]
            for t in range(PACK):
                nc.vector.tensor_tensor(sums[:, t, :], rows[1][t][:].indirect(entries(dst_t, lo, hi)), fetched[t][lo // HALF][:, lo % HALF : lo % HALF + hi - lo], ADD)

        def activate(z, sums):
            nc.scalar.activation(
                z.rearrange("p (c i) t -> p c t i", i=LINE),
                sums.rearrange("p t (c i) -> p c t i", i=LINE),
                SILU,
            )

        def second_layer(c, z):
            lo, hi = EDGE_CHUNKS[c]
            zq = quantize(z.rearrange("p n j -> p (n j)"), hi - lo, f"z{c}")
            bank = psum.tile([P, hi - lo], F32, name="out_bank", tag=f"bank{c}")
            product(bank[:], (w3_codes, w3_bytes), slice(0, N), zq, 0, hi - lo)
            result = keep.tile([P, hi - lo], F32, name=f"result{c}")
            nc.scalar.copy(result[:], bank[:])
            nc.sync.dma_start(out=out[:, lo:hi], in_=result[:])

        sums0 = keep.tile([P, PACK, 512], F32, name="sums0")
        z0 = keep.tile([P, 512, PACK], BF16, name="z0", tag="z0", align_bytes=64)
        join(0, sums0[:])
        activate(z0[:], sums0[:])
        sums1 = keep.tile([P, PACK, 288], F32, name="sums1", tag="fetched30")
        z_rest = keep.tile([P, 512, PACK], BF16, name="z_rest", align_bytes=64)
        join(1, sums1[:])
        activate(z_rest[:, 0:288], sums1[:])
        second_layer(0, z0[:])
        sums23 = keep.tile([P, PACK * 224], F32, name="sums23", tag="z0", align_bytes=64)
        sums2 = sums23[:, 0 : PACK * 160].rearrange("p (t n) -> p t n", t=PACK)
        sums3 = sums23[:, PACK * 160 :].rearrange("p (t n) -> p t n", t=PACK)
        join(2, sums2)
        activate(z_rest[:, 288:448], sums2)
        join(3, sums3)
        activate(z_rest[:, 448:512], sums3)
        second_layer(1, z_rest[:, 0:256])
        second_layer(2, z_rest[:, 256:384])
        second_layer(3, z_rest[:, 384:512])
